import numpy as np
import ml_dtypes

BF16 = ml_dtypes.bfloat16


def bf(x):
    return np.asarray(x, np.float32).astype(BF16)


def f32(x):
    return np.asarray(x, np.float32)


def f64(x):
    return np.asarray(x).astype(np.float64)


def striped(idx):
    return np.tile(idx.reshape(-1, 16).T, (8, 1))


S, K, M, N = 512, 128, 256, 64


def setup_inputs():
    return {"base": bf(np.random.standard_normal((M, S))), "x": bf(np.random.standard_normal((K, N))), "w": bf(np.random.standard_normal((K, M)) / np.sqrt(K)), "offs": striped(np.random.permutation(S)[:N])}


def reference(base, x, w, offs):
    idx = offs[:16].T.reshape(-1)
    z = f64(base).copy()
    z[:, idx] += f64(w).T @ f64(x)
    return z

@@ -1,0 +1,48 @@
+import concourse.mybir as mybir
+from concourse.masks import make_identity
+
+BF16, F32, U16 = mybir.dt.bfloat16, mybir.dt.float32, mybir.dt.uint16
+
+P = 128
+S, M, N = 512, 256, 64
+BLOCKS = M // P
+
+FLOPS = 2 * P * M * N
+
+
+def tile_scatter_matmul_kernel(tc, base, x, w, offs, out):
+    nc = tc.nc
+    with (
+        tc.tile_pool(name="held", bufs=1) as held,
+        tc.psum_pool(name="psum", bufs=1) as psum,
+    ):
+        base_tile = held.tile([P, BLOCKS, S], BF16)
+        weights = held.tile([P, M], BF16)
+        moving = held.tile([P, N], BF16)
+        offsets = held.tile([P, N // 16], U16)
+        nc.sync.dma_start(base_tile[:], base.rearrange("(b p) s -> p b s", p=P))
+        nc.sync.dma_start(offsets[:], offs)
+        nc.scalar.dma_start(weights[:], w)
+        nc.scalar.dma_start(moving[:], x)
+
+        ident = held.tile([P, P], BF16)
+        make_identity(nc, ident[:])
+
+        windows = [psum.tile([P, S], F32, name=f"window{b}") for b in range(BLOCKS)]
+        for b in range(BLOCKS):
+            nc.tensor.matmul(windows[b][:], ident[:], base_tile[:, b, :], start=True, stop=False)
+
+        for b in range(BLOCKS):
+            nc.tensor.matmul(
+                windows[b][:].indirect(offsets[:]),
+                weights[:, b * P : (b + 1) * P],
+                moving[:],
+                start=False,
+                stop=True,
+            )
+
+        out_tiles = [held.tile([P, S], F32, name=f"out_tile{b}") for b in range(BLOCKS)]
+        nc.vector.tensor_copy(out_tiles[0][:], windows[0][:])
+        nc.sync.dma_start(out[0:P, :], out_tiles[0][:])
+        nc.scalar.copy(out_tiles[1][:], windows[1][:])
+        nc.scalar.dma_start(out[P : 2 * P, :], out_tiles[1][:])

@@ -20,10 +20,11 @@ def tile_scatter_matmul_kernel(tc, base, x, w, offs, out):
         weights = held.tile([P, M], BF16)
         moving = held.tile([P, N], BF16)
         offsets = held.tile([P, N // 16], U16)
-        nc.sync.dma_start(base_tile[:], base.rearrange("(b p) s -> p b s", p=P))
+        nc.sync.dma_start(base_tile[:, 0, :], base[0:P, :])
+        nc.scalar.dma_start(base_tile[:, 1, :], base[P : 2 * P, :])
         nc.sync.dma_start(offsets[:], offs)
         nc.scalar.dma_start(weights[:], w)
-        nc.scalar.dma_start(moving[:], x)
+        nc.sync.dma_start(moving[:], x)
 
         ident = held.tile([P, P], BF16)
         make_identity(nc, ident[:])

@@ -7,6 +7,8 @@ P = 128
 S, M, N = 512, 256, 64
 BLOCKS = M // P
 
+WARM_UPS = 12
+
 FLOPS = 2 * P * M * N
 
 
@@ -25,6 +27,12 @@ def tile_scatter_matmul_kernel(tc, base, x, w, offs, out):
         nc.sync.dma_start(offsets[:], offs)
         nc.scalar.dma_start(weights[:], w)
         nc.sync.dma_start(moving[:], x)
+
+        zeros = held.tile([P, P], BF16)
+        nc.vector.memset(zeros[:], 0.0)
+        spare = psum.tile([P, P], F32)
+        for warm_up in range(WARM_UPS):
+            nc.tensor.matmul(spare[:], zeros[:], zeros[:], start=True, stop=True)
 
         ident = held.tile([P, P], BF16)
         make_identity(nc, ident[:])

import concourse.mybir as mybir
from concourse.masks import make_identity

BF16, F32, U16 = mybir.dt.bfloat16, mybir.dt.float32, mybir.dt.uint16

P = 128
S, M, N = 512, 256, 64
BLOCKS = M // P

WARM_UPS = 12

FLOPS = 2 * P * M * N


def tile_scatter_matmul_kernel(tc, base, x, w, offs, out):
    nc = tc.nc
    with (
        tc.tile_pool(name="held", bufs=1) as held,
        tc.psum_pool(name="psum", bufs=1) as psum,
    ):
        base_tile = held.tile([P, BLOCKS, S], BF16)
        weights = held.tile([P, M], BF16)
        moving = held.tile([P, N], BF16)
        offsets = held.tile([P, N // 16], U16)
        nc.sync.dma_start(base_tile[:, 0, :], base[0:P, :])
        nc.scalar.dma_start(base_tile[:, 1, :], base[P : 2 * P, :])
        nc.sync.dma_start(offsets[:], offs)
        nc.scalar.dma_start(weights[:], w)
        nc.sync.dma_start(moving[:], x)

        zeros = held.tile([P, P], BF16)
        nc.vector.memset(zeros[:], 0.0)
        spare = psum.tile([P, P], F32)
        for warm_up in range(WARM_UPS):
            nc.tensor.matmul(spare[:], zeros[:], zeros[:], start=True, stop=True)

        ident = held.tile([P, P], BF16)
        make_identity(nc, ident[:])

        windows = [psum.tile([P, S], F32, name=f"window{b}") for b in range(BLOCKS)]
        for b in range(BLOCKS):
            nc.tensor.matmul(windows[b][:], ident[:], base_tile[:, b, :], start=True, stop=False)

        for b in range(BLOCKS):
            nc.tensor.matmul(
                windows[b][:].indirect(offsets[:]),
                weights[:, b * P : (b + 1) * P],
                moving[:],
                start=False,
                stop=True,
            )

        out_tiles = [held.tile([P, S], F32, name=f"out_tile{b}") for b in range(BLOCKS)]
        nc.vector.tensor_copy(out_tiles[0][:], windows[0][:])
        nc.sync.dma_start(out[0:P, :], out_tiles[0][:])
        nc.scalar.copy(out_tiles[1][:], windows[1][:])
        nc.scalar.dma_start(out[P : 2 * P, :], out_tiles[1][:])
